import numpy as np
import ml_dtypes

BF16 = ml_dtypes.bfloat16


def bf(x):
    return np.asarray(x, np.float32).astype(BF16)


def f32(x):
    return np.asarray(x, np.float32)


def f64(x):
    return np.asarray(x).astype(np.float64)


def striped(idx):
    return np.tile(idx.reshape(-1, 16).T, (8, 1))


def rows(idx, k):
    return np.tile(idx, (k, 1))


def look(tab, idx):
    return np.take_along_axis(f64(tab), rows(idx, len(tab)), axis=1)


K, S, V, N = 256, 2048, 512, 512


def setup_inputs():
    return {"tab": f32(np.random.standard_normal((2, K, S))), "y": f32(np.random.standard_normal((K, V))), "offs": striped(np.random.permutation(S)[:N])}


def reference(tab, y, offs):
    idx = offs[:16].T.reshape(-1)
    x = (look(tab[0], idx) * f64(y)) * (np.tanh(look(tab[1], idx)))
    return x

@@ -1,0 +1,36 @@
+import concourse.mybir as mybir
+
+F32, U16 = mybir.dt.float32, mybir.dt.uint16
+MULT = mybir.AluOpType.mult
+TANH = mybir.ActivationFunctionType.Tanh
+P = 128
+
+
+def tile_lookup_vg_multanh_out_kernel(tc, tab, y, offs, out):
+    nc = tc.nc
+    rows, picked = y.shape
+    places = tab.shape[2]
+    blocks = rows // P
+
+    with tc.tile_pool(name="held", bufs=1) as held, tc.tile_pool(name="work", bufs=2) as work:
+        offsets = held.tile([P, picked // 16], U16, name="offsets")
+        nc.sync.dma_start(offsets[:], offs)
+
+        gates, streams, values = [], [], []
+        for b in range(blocks):
+            block = slice(b * P, (b + 1) * P)
+            gates.append(held.tile([P, places], F32, name=f"gates{b}"))
+            streams.append(held.tile([P, picked], F32, name=f"stream{b}"))
+            values.append(held.tile([P, places], F32, name=f"values{b}"))
+            nc.sync.dma_start(gates[b][:], tab[1, block, :])
+            nc.sync.dma_start(streams[b][:], y[block, :])
+            nc.sync.dma_start(values[b][:], tab[0, block, :])
+
+        for b in range(blocks):
+            gate = work.tile([P, picked], F32, name="gate")
+            nc.scalar.activation(gate[:], gates[b][:].indirect(offsets[:]), TANH)
+            product = work.tile([P, picked], F32, name="product")
+            nc.vector.tensor_tensor(product[:], values[b][:].indirect(offsets[:]), streams[b][:], MULT)
+            result = work.tile([P, picked], F32, name="result")
+            nc.vector.tensor_tensor(result[:], product[:], gate[:], MULT)
+            nc.sync.dma_start(out[b * P : (b + 1) * P, :], result[:])

@@ -29,8 +29,8 @@ def tile_lookup_vg_multanh_out_kernel(tc, tab, y, offs, out):
         for b in range(blocks):
             gate = work.tile([P, picked], F32, name="gate")
             nc.scalar.activation(gate[:], gates[b][:].indirect(offsets[:]), TANH)
-            product = work.tile([P, picked], F32, name="product")
-            nc.vector.tensor_tensor(product[:], values[b][:].indirect(offsets[:]), streams[b][:], MULT)
+            gated_stream = work.tile([P, picked], F32, name="gated_stream")
+            nc.vector.tensor_tensor(gated_stream[:], streams[b][:], gate[:], MULT)
             result = work.tile([P, picked], F32, name="result")
-            nc.vector.tensor_tensor(result[:], product[:], gate[:], MULT)
+            nc.vector.tensor_tensor(result[:], values[b][:].indirect(offsets[:]), gated_stream[:], MULT)
             nc.sync.dma_start(out[b * P : (b + 1) * P, :], result[:])

@@ -32,5 +32,10 @@ def tile_lookup_vg_multanh_out_kernel(tc, tab, y, offs, out):
             gated_stream = work.tile([P, picked], F32, name="gated_stream")
             nc.vector.tensor_tensor(gated_stream[:], streams[b][:], gate[:], MULT)
             result = work.tile([P, picked], F32, name="result")
-            nc.vector.tensor_tensor(result[:], values[b][:].indirect(offsets[:]), gated_stream[:], MULT)
-            nc.sync.dma_start(out[b * P : (b + 1) * P, :], result[:])
+            for k in range(2):
+                piece = slice(k * picked // 2, (k + 1) * picked // 2)
+                places_of_piece = offsets[:, k * picked // 32 : (k + 1) * picked // 32]
+                nc.vector.tensor_tensor(
+                    result[:, piece], values[b][:].indirect(places_of_piece), gated_stream[:, piece], MULT
+                )
+                nc.sync.dma_start(out[b * P : (b + 1) * P, piece], result[:, piece])

@@ -11,31 +11,35 @@ def tile_lookup_vg_multanh_out_kernel(tc, tab, y, offs, out):
     rows, picked = y.shape
     places = tab.shape[2]
     blocks = rows // P
+    table_rows = tab.rearrange("t (p b) s -> t b p s", b=blocks)
+    stream_rows = y.rearrange("(p b) v -> p b v", b=blocks)
+    out_rows = out.rearrange("(p b) v -> b p v", b=blocks)
 
     with tc.tile_pool(name="held", bufs=1) as held, tc.tile_pool(name="work", bufs=2) as work:
         offsets = held.tile([P, picked // 16], U16, name="offsets")
         nc.sync.dma_start(offsets[:], offs)
 
-        gates, streams, values = [], [], []
+        gates = [held.tile([P, places], F32, name=f"gates{b}") for b in range(blocks)]
+        stream = held.tile([P, blocks, picked], F32, name="stream")
+        values = [held.tile([P, places], F32, name=f"values{b}") for b in range(blocks)]
         for b in range(blocks):
-            block = slice(b * P, (b + 1) * P)
-            gates.append(held.tile([P, places], F32, name=f"gates{b}"))
-            streams.append(held.tile([P, picked], F32, name=f"stream{b}"))
-            values.append(held.tile([P, places], F32, name=f"values{b}"))
-            nc.sync.dma_start(gates[b][:], tab[1, block, :])
-            nc.sync.dma_start(streams[b][:], y[block, :])
-            nc.sync.dma_start(values[b][:], tab[0, block, :])
+            nc.sync.dma_start(gates[b][:], table_rows[1, b])
+        nc.sync.dma_start(stream[:], stream_rows)
+        for b in range(blocks):
+            nc.sync.dma_start(values[b][:], table_rows[0, b])
 
+        gated_stream = held.tile([P, blocks, picked], F32, name="gated_stream")
         for b in range(blocks):
             gate = work.tile([P, picked], F32, name="gate")
             nc.scalar.activation(gate[:], gates[b][:].indirect(offsets[:]), TANH)
-            gated_stream = work.tile([P, picked], F32, name="gated_stream")
-            nc.vector.tensor_tensor(gated_stream[:], streams[b][:], gate[:], MULT)
+            nc.vector.tensor_tensor(gated_stream[:, b], stream[:, b], gate[:], MULT)
+
+        for b in range(blocks):
             result = work.tile([P, picked], F32, name="result")
             for k in range(2):
                 piece = slice(k * picked // 2, (k + 1) * picked // 2)
-                places_of_piece = offsets[:, k * picked // 32 : (k + 1) * picked // 32]
+                list_columns = offsets[:, k * picked // 32 : (k + 1) * picked // 32]
                 nc.vector.tensor_tensor(
-                    result[:, piece], values[b][:].indirect(places_of_piece), gated_stream[:, piece], MULT
+                    result[:, piece], values[b][:].indirect(list_columns), gated_stream[:, b, piece], MULT
                 )
-                nc.sync.dma_start(out[b * P : (b + 1) * P, piece], result[:, piece])
+                nc.sync.dma_start(out_rows[b, :, piece], result[:, piece])

import concourse.mybir as mybir

F32, U16 = mybir.dt.float32, mybir.dt.uint16
MULT = mybir.AluOpType.mult
TANH = mybir.ActivationFunctionType.Tanh
P = 128


def tile_lookup_vg_multanh_out_kernel(tc, tab, y, offs, out):
    nc = tc.nc
    rows, picked = y.shape
    places = tab.shape[2]
    blocks = rows // P
    table_rows = tab.rearrange("t (p b) s -> t b p s", b=blocks)
    stream_rows = y.rearrange("(p b) v -> p b v", b=blocks)
    out_rows = out.rearrange("(p b) v -> b p v", b=blocks)

    with tc.tile_pool(name="held", bufs=1) as held, tc.tile_pool(name="work", bufs=2) as work:
        offsets = held.tile([P, picked // 16], U16, name="offsets")
        nc.sync.dma_start(offsets[:], offs)

        gates = [held.tile([P, places], F32, name=f"gates{b}") for b in range(blocks)]
        stream = held.tile([P, blocks, picked], F32, name="stream")
        values = [held.tile([P, places], F32, name=f"values{b}") for b in range(blocks)]
        for b in range(blocks):
            nc.sync.dma_start(gates[b][:], table_rows[1, b])
        nc.sync.dma_start(stream[:], stream_rows)
        for b in range(blocks):
            nc.sync.dma_start(values[b][:], table_rows[0, b])

        gated_stream = held.tile([P, blocks, picked], F32, name="gated_stream")
        for b in range(blocks):
            gate = work.tile([P, picked], F32, name="gate")
            nc.scalar.activation(gate[:], gates[b][:].indirect(offsets[:]), TANH)
            nc.vector.tensor_tensor(gated_stream[:, b], stream[:, b], gate[:], MULT)

        for b in range(blocks):
            result = work.tile([P, picked], F32, name="result")
            for k in range(2):
                piece = slice(k * picked // 2, (k + 1) * picked // 2)
                list_columns = offsets[:, k * picked // 32 : (k + 1) * picked // 32]
                nc.vector.tensor_tensor(
                    result[:, piece], values[b][:].indirect(list_columns), gated_stream[:, b, piece], MULT
                )
                nc.sync.dma_start(out_rows[b, :, piece], result[:, piece])
